import numpy as np
CORES = [0,1,2,3,4,5,6,7,8,9,10,11,12,13,14,15]
N = 16
ROUNDS = 4
def setup_inputs(rng):
    return {"x": rng.standard_normal((N, ROUNDS, 128, 64), dtype=np.float32)}
def reference(x):
    b = 64 // N
    bl = x.reshape(N, ROUNDS, 128, N, b)
    return {"y": np.ascontiguousarray(bl.transpose(3, 1, 2, 0, 4)).reshape(N, ROUNDS, 128, 64)}

@@ -1,0 +1,84 @@
+import concourse.bass as bass
+
+SCRATCH = {
+    "S": ("sbuf", [128, 64], "float32"),
+    "L": ("sbuf", [128, 64], "float32"),
+    "R": ("sbuf", [128, 64], "float32"),
+}
+SEMAPHORES = ["ld", "st", "ownl", "ownr", "sent", "x2l", "rarr", "oarr", "xarr", "ready", "xcred", "sig"]
+GW = (2, 3, 6, 7)
+ROUNDS = 4
+
+
+def rank_program(g, core, T, topo):
+    if T.rank_of(core) is None:
+        return
+    ch, i = divmod(core, 8)
+    base, ob = 8 * ch, 8 * (1 - ch)
+    gw = i in GW
+    peers = [base + j for j in range(8) if j != i]
+    sem = T.sem
+
+    def dst(c):
+        a = topo.addr(c)
+        return bass.DstId(rid=a[0], pnc=a[1])
+
+    def own_loads(k):
+        g.dma_start(T.L[:, 4 * core:4 * core + 4], T.x[k, :, 4 * core:4 * core + 4]).then_inc(sem.ownl, 16)
+        if gw:
+            for di, j in ((0, i - 2), (1, i)):
+                d = ob + j
+                g.dma_start(T.R[:, 32 * di + 4 * i:32 * di + 4 * i + 4], T.x[k, :, 4 * d:4 * d + 4]).then_inc(sem.ownr, 16)
+
+    nsig = 0
+    g.dma_start(T.S[:], T.x[0]).then_inc(sem.ld, 16)
+    own_loads(0)
+    for k in range(ROUNDS):
+        g.wait_ge(sem.ld, 16 * (k + 1))
+        if k:
+            g.wait_ge(sem.ready, 7 * k)
+            if gw:
+                a = topo.addr(ob + i)
+                g.remote_sem_update(sem.xcred, sem.sig, a[1], a[0], 1)
+                nsig += 1
+        tr = []
+        for p in peers:
+            tr.append(bass.RemoteDMATransfer(dst_ids=[dst(p)], dma_engine_mask=1 << len(tr), remote_sem=sem.oarr,
+                                             src=T.S[:, 4 * p:4 * p + 4], dst=T.L[:, 4 * core:4 * core + 4]))
+        for j in range(8):
+            q = j if j in GW else j + 2
+            if q == i:
+                continue
+            di = 1 if j in GW else 0
+            d = ob + j
+            tr.append(bass.RemoteDMATransfer(dst_ids=[dst(base + q)], dma_engine_mask=1 << len(tr), remote_sem=sem.rarr,
+                                             src=T.S[:, 4 * d:4 * d + 4],
+                                             dst=T.R[:, 32 * di + 4 * i:32 * di + 4 * i + 4]))
+        g.remote_dma_fused(tr, local_sem=sem.sent)
+        nw1 = len(tr)
+        g.wait_ge(sem.sent, nw1 * (k + 1))
+        if k + 1 < ROUNDS:
+            g.dma_start(T.S[:], T.x[k + 1]).then_inc(sem.ld, 16)
+        if gw:
+            g.wait_ge(sem.rarr, 14 * (k + 1))
+            g.wait_ge(sem.ownr, 32 * (k + 1))
+            if k:
+                g.wait_ge(sem.xcred, k)
+            tr = []
+            for di, j in ((0, i - 2), (1, i)):
+                tr.append(bass.RemoteDMATransfer(dst_ids=[dst(ob + j)], dma_engine_mask=0xF << (4 * di), remote_sem=sem.xarr,
+                                                 src=T.R[:, 32 * di:32 * di + 32], dst=T.L[:, 32 * ch:32 * ch + 32]))
+            g.remote_dma_fused(tr, local_sem=sem.x2l)
+        g.wait_ge(sem.oarr, 7 * (k + 1))
+        g.wait_ge(sem.xarr, 4 * (k + 1))
+        g.wait_ge(sem.ownl, 16 * (k + 1))
+        g.dma_start(T.y[k], T.L[:]).then_inc(sem.st, 16)
+        g.wait_ge(sem.st, 16 * (k + 1))
+        if gw:
+            g.wait_ge(sem.x2l, 8 * (k + 1))
+        if k + 1 < ROUNDS:
+            own_loads(k + 1)
+            g.remote_dma_fused([bass.RemoteDMATransfer(dst_ids=[dst(p)], dma_engine_mask=1 << n, remote_sem=sem.ready)
+                                for n, p in enumerate(peers)], local_sem=sem.sig)
+            nsig += 7
+    g.wait_ge(sem.sig, nsig)

@@ -5,7 +5,8 @@ SCRATCH = {
     "L": ("sbuf", [128, 64], "float32"),
     "R": ("sbuf", [128, 64], "float32"),
 }
-SEMAPHORES = ["ld", "st", "ownl", "ownr", "sent", "x2l", "rarr", "oarr", "xarr", "ready", "xcred", "sig"]
+SEMAPHORES = ["ld", "st", "ownl", "ownr", "sent", "x2l", "rarr", "oarr0", "oarr1", "xarr0", "xarr1",
+              "rcred", "lcred", "xcred", "pst0", "pst1", "sig"]
 GW = (2, 3, 6, 7)
 ROUNDS = 4
 
@@ -17,68 +18,93 @@ def rank_program(g, core, T, topo):
     base, ob = 8 * ch, 8 * (1 - ch)
     gw = i in GW
     peers = [base + j for j in range(8) if j != i]
+    ngw = 3 if gw else 4
     sem = T.sem
+    oarr = (sem.oarr0, sem.oarr1)
+    xarr = (sem.xarr0, sem.xarr1)
+    pst = (sem.pst0, sem.pst1)
 
     def dst(c):
         a = topo.addr(c)
         return bass.DstId(rid=a[0], pnc=a[1])
 
-    def own_loads(k):
-        g.dma_start(T.L[:, 4 * core:4 * core + 4], T.x[k, :, 4 * core:4 * core + 4]).then_inc(sem.ownl, 16)
-        if gw:
-            for di, j in ((0, i - 2), (1, i)):
-                d = ob + j
-                g.dma_start(T.R[:, 32 * di + 4 * i:32 * di + 4 * i + 4], T.x[k, :, 4 * d:4 * d + 4]).then_inc(sem.ownr, 16)
+    def land(c, k):
+        return T.R if (c % 8 not in GW and k % 2) else T.L
+
+    def own_l(k):
+        g.dma_start(land(core, k)[:, 4 * core:4 * core + 4], T.x[k, :, 4 * core:4 * core + 4]).then_inc(sem.ownl, 16)
+
+    def own_r(k):
+        for di, j in ((0, i - 2), (1, i)):
+            d = ob + j
+            g.dma_start(T.R[:, 32 * di + 4 * i:32 * di + 4 * i + 4], T.x[k, :, 4 * d:4 * d + 4]).then_inc(sem.ownr, 16)
 
     nsig = 0
+    nsent = 0
     g.dma_start(T.S[:], T.x[0]).then_inc(sem.ld, 16)
-    own_loads(0)
+    if gw:
+        own_r(0)
+    own_l(0)
     for k in range(ROUNDS):
         g.wait_ge(sem.ld, 16 * (k + 1))
         if k:
-            g.wait_ge(sem.ready, 7 * k)
-            if gw:
-                a = topo.addr(ob + i)
-                g.remote_sem_update(sem.xcred, sem.sig, a[1], a[0], 1)
-                nsig += 1
+            g.wait_ge(sem.rcred, ngw * k)
         tr = []
-        for p in peers:
-            tr.append(bass.RemoteDMATransfer(dst_ids=[dst(p)], dma_engine_mask=1 << len(tr), remote_sem=sem.oarr,
-                                             src=T.S[:, 4 * p:4 * p + 4], dst=T.L[:, 4 * core:4 * core + 4]))
         for j in range(8):
             q = j if j in GW else j + 2
             if q == i:
                 continue
             di = 1 if j in GW else 0
             d = ob + j
-            tr.append(bass.RemoteDMATransfer(dst_ids=[dst(base + q)], dma_engine_mask=1 << len(tr), remote_sem=sem.rarr,
+            tr.append(bass.RemoteDMATransfer(dst_ids=[dst(base + q)], dma_engine_mask=3 << (2 * len(tr)), remote_sem=sem.rarr,
                                              src=T.S[:, 4 * d:4 * d + 4],
                                              dst=T.R[:, 32 * di + 4 * i:32 * di + 4 * i + 4]))
         g.remote_dma_fused(tr, local_sem=sem.sent)
-        nw1 = len(tr)
-        g.wait_ge(sem.sent, nw1 * (k + 1))
-        if k + 1 < ROUNDS:
-            g.dma_start(T.S[:], T.x[k + 1]).then_inc(sem.ld, 16)
+        nsent += 2 * len(tr)
+        if k:
+            g.wait_ge(sem.st, 16 * k)
+            own_l(k)
+            if gw:
+                if k >= 2:
+                    g.wait_ge(pst[k - 2], 1)
+                sg = [bass.RemoteDMATransfer(dst_ids=[dst(p)], dma_engine_mask=1 << (8 + n), remote_sem=sem.lcred)
+                      for n, p in enumerate(peers)]
+                sg.append(bass.RemoteDMATransfer(dst_ids=[dst(ob + i)], dma_engine_mask=1, remote_sem=sem.xcred))
+                g.remote_dma_fused(sg, local_sem=sem.sig)
+                nsig += 8
+            elif k <= 2:
+                a = topo.addr(core + 2)
+                g.remote_sem_update(pst[k - 1], sem.sig, a[1], a[0], 1)
+                nsig += 1
+            g.wait_ge(sem.lcred, ngw * k)
+        tr = [bass.RemoteDMATransfer(dst_ids=[dst(p)], dma_engine_mask=3 << (2 + 2 * n), remote_sem=oarr[k % 2],
+                                     src=T.S[:, 4 * p:4 * p + 4], dst=land(p, k)[:, 4 * core:4 * core + 4])
+              for n, p in enumerate(peers)]
+        g.remote_dma_fused(tr, local_sem=sem.sent)
+        nsent += 14
         if gw:
-            g.wait_ge(sem.rarr, 14 * (k + 1))
+            g.wait_ge(sem.rarr, 28 * (k + 1))
             g.wait_ge(sem.ownr, 32 * (k + 1))
             if k:
                 g.wait_ge(sem.xcred, k)
             tr = []
             for di, j in ((0, i - 2), (1, i)):
-                tr.append(bass.RemoteDMATransfer(dst_ids=[dst(ob + j)], dma_engine_mask=0xF << (4 * di), remote_sem=sem.xarr,
-                                                 src=T.R[:, 32 * di:32 * di + 32], dst=T.L[:, 32 * ch:32 * ch + 32]))
+                tr.append(bass.RemoteDMATransfer(dst_ids=[dst(ob + j)], dma_engine_mask=0xF << (4 * di), remote_sem=xarr[k % 2],
+                                                 src=T.R[:, 32 * di:32 * di + 32], dst=land(ob + j, k)[:, 32 * ch:32 * ch + 32]))
             g.remote_dma_fused(tr, local_sem=sem.x2l)
-        g.wait_ge(sem.oarr, 7 * (k + 1))
-        g.wait_ge(sem.xarr, 4 * (k + 1))
-        g.wait_ge(sem.ownl, 16 * (k + 1))
-        g.dma_start(T.y[k], T.L[:]).then_inc(sem.st, 16)
-        g.wait_ge(sem.st, 16 * (k + 1))
+        g.wait_ge(sem.sent, nsent)
+        if k + 1 < ROUNDS:
+            g.dma_start(T.S[:], T.x[k + 1]).then_inc(sem.ld, 16)
         if gw:
             g.wait_ge(sem.x2l, 8 * (k + 1))
-        if k + 1 < ROUNDS:
-            own_loads(k + 1)
-            g.remote_dma_fused([bass.RemoteDMATransfer(dst_ids=[dst(p)], dma_engine_mask=1 << n, remote_sem=sem.ready)
-                                for n, p in enumerate(peers)], local_sem=sem.sig)
-            nsig += 7
+            if k + 1 < ROUNDS:
+                own_r(k + 1)
+                g.remote_dma_fused([bass.RemoteDMATransfer(dst_ids=[dst(p)], dma_engine_mask=1 << n, remote_sem=sem.rcred)
+                                    for n, p in enumerate(peers)], local_sem=sem.sig)
+                nsig += 7
+        g.wait_ge(oarr[k % 2], 14 * (k // 2 + 1))
+        g.wait_ge(xarr[k % 2], 4 * (k // 2 + 1))
+        g.wait_ge(sem.ownl, 16 * (k + 1))
+        g.dma_start(T.y[k], land(core, k)[:]).then_inc(sem.st, 16)
+    g.wait_ge(sem.st, 16 * ROUNDS)
     g.wait_ge(sem.sig, nsig)

@@ -2,12 +2,13 @@ import concourse.bass as bass
 
 SCRATCH = {
     "S": ("sbuf", [128, 64], "float32"),
-    "L": ("sbuf", [128, 64], "float32"),
-    "R": ("sbuf", [128, 64], "float32"),
+    "L": ("sbuf", [128, 2, 32], "float32"),
+    "R": ("sbuf", [128, 2, 32], "float32"),
 }
 SEMAPHORES = ["ld", "st", "ownl", "ownr", "sent", "x2l", "rarr", "oarr0", "oarr1", "xarr0", "xarr1",
-              "rcred", "lcred", "xcred", "pst0", "pst1", "sig"]
+              "rcred", "lcred", "xcred", "ycred0", "ycred1", "pst0", "pst1", "sig"]
 GW = (2, 3, 6, 7)
+SERVER = (2, 2, 3, 3, 6, 6, 7, 7)
 ROUNDS = 4
 
 
@@ -17,12 +18,14 @@ def rank_program(g, core, T, topo):
     ch, i = divmod(core, 8)
     base, ob = 8 * ch, 8 * (1 - ch)
     gw = i in GW
+    relay = i in (2, 6)
     peers = [base + j for j in range(8) if j != i]
     ngw = 3 if gw else 4
     sem = T.sem
     oarr = (sem.oarr0, sem.oarr1)
     xarr = (sem.xarr0, sem.xarr1)
     pst = (sem.pst0, sem.pst1)
+    ycred = (sem.ycred0, sem.ycred1)
 
     def dst(c):
         a = topo.addr(c)
@@ -32,12 +35,11 @@ def rank_program(g, core, T, topo):
         return T.R if (c % 8 not in GW and k % 2) else T.L
 
     def own_l(k):
-        g.dma_start(land(core, k)[:, 4 * core:4 * core + 4], T.x[k, :, 4 * core:4 * core + 4]).then_inc(sem.ownl, 16)
+        g.dma_start(land(core, k)[:, ch, 4 * i:4 * i + 4], T.x[k, :, 4 * core:4 * core + 4]).then_inc(sem.ownl, 16)
 
     def own_r(k):
-        for di, j in ((0, i - 2), (1, i)):
-            d = ob + j
-            g.dma_start(T.R[:, 32 * di + 4 * i:32 * di + 4 * i + 4], T.x[k, :, 4 * d:4 * d + 4]).then_inc(sem.ownr, 16)
+        d = ob + SERVER.index(i)
+        g.dma_start(T.R[:, :, 4 * i:4 * i + 4], T.x[k, :, 4 * d:4 * d + 8]).then_inc(sem.ownr, 16)
 
     nsig = 0
     nsent = 0
@@ -51,46 +53,47 @@ def rank_program(g, core, T, topo):
             g.wait_ge(sem.rcred, ngw * k)
         tr = []
         for j in range(8):
-            q = j if j in GW else j + 2
-            if q == i:
+            if SERVER[j] == i:
                 continue
-            di = 1 if j in GW else 0
             d = ob + j
-            tr.append(bass.RemoteDMATransfer(dst_ids=[dst(base + q)], dma_engine_mask=3 << (2 * len(tr)), remote_sem=sem.rarr,
-                                             src=T.S[:, 4 * d:4 * d + 4],
-                                             dst=T.R[:, 32 * di + 4 * i:32 * di + 4 * i + 4]))
+            tr.append(bass.RemoteDMATransfer(dst_ids=[dst(base + SERVER[j])], dma_engine_mask=3 << (2 * len(tr)),
+                                             remote_sem=sem.rarr, src=T.S[:, 4 * d:4 * d + 4],
+                                             dst=T.R[:, j % 2, 4 * i:4 * i + 4]))
         g.remote_dma_fused(tr, local_sem=sem.sent)
         nsent += 2 * len(tr)
         if k:
             g.wait_ge(sem.st, 16 * k)
-            own_l(k)
             if gw:
-                if k >= 2:
-                    g.wait_ge(pst[k - 2], 1)
                 sg = [bass.RemoteDMATransfer(dst_ids=[dst(p)], dma_engine_mask=1 << (8 + n), remote_sem=sem.lcred)
                       for n, p in enumerate(peers)]
-                sg.append(bass.RemoteDMATransfer(dst_ids=[dst(ob + i)], dma_engine_mask=1, remote_sem=sem.xcred))
+                sg.append(bass.RemoteDMATransfer(dst_ids=[dst(ob + SERVER[i])], dma_engine_mask=1, remote_sem=sem.xcred))
+                if relay and k >= 2:
+                    g.wait_ge(pst[k - 2], 2)
+                    sg.append(bass.RemoteDMATransfer(dst_ids=[dst(ob + i)], dma_engine_mask=2, remote_sem=ycred[k - 2]))
                 g.remote_dma_fused(sg, local_sem=sem.sig)
-                nsig += 8
+                nsig += len(sg)
             elif k <= 2:
-                a = topo.addr(core + 2)
+                a = topo.addr(base + SERVER[i])
                 g.remote_sem_update(pst[k - 1], sem.sig, a[1], a[0], 1)
                 nsig += 1
+            own_l(k)
             g.wait_ge(sem.lcred, ngw * k)
         tr = [bass.RemoteDMATransfer(dst_ids=[dst(p)], dma_engine_mask=3 << (2 + 2 * n), remote_sem=oarr[k % 2],
-                                     src=T.S[:, 4 * p:4 * p + 4], dst=land(p, k)[:, 4 * core:4 * core + 4])
+                                     src=T.S[:, 4 * p:4 * p + 4], dst=land(p, k)[:, ch, 4 * i:4 * i + 4])
               for n, p in enumerate(peers)]
         g.remote_dma_fused(tr, local_sem=sem.sent)
         nsent += 14
         if gw:
             g.wait_ge(sem.rarr, 28 * (k + 1))
-            g.wait_ge(sem.ownr, 32 * (k + 1))
-            if k:
-                g.wait_ge(sem.xcred, k)
-            tr = []
-            for di, j in ((0, i - 2), (1, i)):
-                tr.append(bass.RemoteDMATransfer(dst_ids=[dst(ob + j)], dma_engine_mask=0xF << (4 * di), remote_sem=xarr[k % 2],
-                                                 src=T.R[:, 32 * di:32 * di + 32], dst=land(ob + j, k)[:, 32 * ch:32 * ch + 32]))
+            g.wait_ge(sem.ownr, 16 * (k + 1))
+            if relay:
+                if k >= 2:
+                    g.wait_ge(ycred[k - 2], 1)
+            elif k:
+                g.wait_ge(sem.xcred, 2 * k)
+            d = ob + SERVER.index(i)
+            tr = [bass.RemoteDMATransfer(dst_ids=[dst(d + h)], dma_engine_mask=0xF << (4 * h), remote_sem=xarr[k % 2],
+                                         src=T.R[:, h, :], dst=land(d + h, k)[:, ch, :]) for h in range(2)]
             g.remote_dma_fused(tr, local_sem=sem.x2l)
         g.wait_ge(sem.sent, nsent)
         if k + 1 < ROUNDS:
@@ -98,10 +101,10 @@ def rank_program(g, core, T, topo):
         if gw:
             g.wait_ge(sem.x2l, 8 * (k + 1))
             if k + 1 < ROUNDS:
-                own_r(k + 1)
                 g.remote_dma_fused([bass.RemoteDMATransfer(dst_ids=[dst(p)], dma_engine_mask=1 << n, remote_sem=sem.rcred)
                                     for n, p in enumerate(peers)], local_sem=sem.sig)
                 nsig += 7
+                own_r(k + 1)
         g.wait_ge(oarr[k % 2], 14 * (k // 2 + 1))
         g.wait_ge(xarr[k % 2], 4 * (k // 2 + 1))
         g.wait_ge(sem.ownl, 16 * (k + 1))

@@ -5,7 +5,7 @@ SCRATCH = {
     "L": ("sbuf", [128, 2, 32], "float32"),
     "R": ("sbuf", [128, 2, 32], "float32"),
 }
-SEMAPHORES = ["ld", "st", "ownl", "ownr", "sent", "x2l", "rarr", "oarr0", "oarr1", "xarr0", "xarr1",
+SEMAPHORES = ["ld", "st", "ownl", "ownr", "fix", "sent", "x2l", "rarr", "oarr0", "oarr1", "xarr0", "xarr1",
               "rcred", "lcred", "xcred", "ycred0", "ycred1", "pst0", "pst1", "sig"]
 GW = (2, 3, 6, 7)
 SERVER = (2, 2, 3, 3, 6, 6, 7, 7)
@@ -26,6 +26,7 @@ def rank_program(g, core, T, topo):
     xarr = (sem.xarr0, sem.xarr1)
     pst = (sem.pst0, sem.pst1)
     ycred = (sem.ycred0, sem.ycred1)
+    own = slice(4 * core, 4 * core + 4)
 
     def dst(c):
         a = topo.addr(c)
@@ -33,9 +34,6 @@ def rank_program(g, core, T, topo):
 
     def land(c, k):
         return T.R if (c % 8 not in GW and k % 2) else T.L
-
-    def own_l(k):
-        g.dma_start(land(core, k)[:, ch, 4 * i:4 * i + 4], T.x[k, :, 4 * core:4 * core + 4]).then_inc(sem.ownl, 16)
 
     def own_r(k):
         d = ob + SERVER.index(i)
@@ -46,7 +44,9 @@ def rank_program(g, core, T, topo):
     g.dma_start(T.S[:], T.x[0]).then_inc(sem.ld, 16)
     if gw:
         own_r(0)
-    own_l(0)
+    kept = (3,) if gw else (2, 3)
+    for k in kept:
+        g.dma_start(land(core, k)[:, ch, 4 * i:4 * i + 4], T.x[k, :, own]).then_inc(sem.ownl, 16)
     for k in range(ROUNDS):
         g.wait_ge(sem.ld, 16 * (k + 1))
         if k:
@@ -76,7 +76,6 @@ def rank_program(g, core, T, topo):
                 a = topo.addr(base + SERVER[i])
                 g.remote_sem_update(pst[k - 1], sem.sig, a[1], a[0], 1)
                 nsig += 1
-            own_l(k)
             g.wait_ge(sem.lcred, ngw * k)
         tr = [bass.RemoteDMATransfer(dst_ids=[dst(p)], dma_engine_mask=3 << (2 + 2 * n), remote_sem=oarr[k % 2],
                                      src=T.S[:, 4 * p:4 * p + 4], dst=land(p, k)[:, ch, 4 * i:4 * i + 4])
@@ -95,6 +94,8 @@ def rank_program(g, core, T, topo):
             tr = [bass.RemoteDMATransfer(dst_ids=[dst(d + h)], dma_engine_mask=0xF << (4 * h), remote_sem=xarr[k % 2],
                                          src=T.R[:, h, :], dst=land(d + h, k)[:, ch, :]) for h in range(2)]
             g.remote_dma_fused(tr, local_sem=sem.x2l)
+        if k == kept[0]:
+            g.dma_start(T.y[0:k, :, own], T.x[0:k, :, own]).then_inc(sem.fix, 16)
         g.wait_ge(sem.sent, nsent)
         if k + 1 < ROUNDS:
             g.dma_start(T.S[:], T.x[k + 1]).then_inc(sem.ld, 16)
@@ -104,10 +105,13 @@ def rank_program(g, core, T, topo):
                 g.remote_dma_fused([bass.RemoteDMATransfer(dst_ids=[dst(p)], dma_engine_mask=1 << n, remote_sem=sem.rcred)
                                     for n, p in enumerate(peers)], local_sem=sem.sig)
                 nsig += 7
-                own_r(k + 1)
         g.wait_ge(oarr[k % 2], 14 * (k // 2 + 1))
         g.wait_ge(xarr[k % 2], 4 * (k // 2 + 1))
-        g.wait_ge(sem.ownl, 16 * (k + 1))
+        if k == 0:
+            g.wait_ge(sem.ownl, 16 * len(kept))
         g.dma_start(T.y[k], land(core, k)[:]).then_inc(sem.st, 16)
+        if gw and k + 1 < ROUNDS:
+            own_r(k + 1)
     g.wait_ge(sem.st, 16 * ROUNDS)
+    g.wait_ge(sem.fix, 16)
     g.wait_ge(sem.sig, nsig)

import concourse.bass as bass

SCRATCH = {
    "S": ("sbuf", [128, 64], "float32"),
    "L": ("sbuf", [128, 2, 32], "float32"),
    "R": ("sbuf", [128, 2, 32], "float32"),
}
SEMAPHORES = ["ld", "st", "ownl", "ownr", "fix", "sent", "x2l", "rarr", "oarr0", "oarr1", "xarr0", "xarr1",
              "rcred", "lcred", "xcred", "ycred0", "ycred1", "pst0", "pst1", "sig"]
GW = (2, 3, 6, 7)
SERVER = (2, 2, 3, 3, 6, 6, 7, 7)
ROUNDS = 4


def rank_program(g, core, T, topo):
    if T.rank_of(core) is None:
        return
    ch, i = divmod(core, 8)
    base, ob = 8 * ch, 8 * (1 - ch)
    gw = i in GW
    relay = i in (2, 6)
    peers = [base + j for j in range(8) if j != i]
    ngw = 3 if gw else 4
    sem = T.sem
    oarr = (sem.oarr0, sem.oarr1)
    xarr = (sem.xarr0, sem.xarr1)
    pst = (sem.pst0, sem.pst1)
    ycred = (sem.ycred0, sem.ycred1)
    own = slice(4 * core, 4 * core + 4)

    def dst(c):
        a = topo.addr(c)
        return bass.DstId(rid=a[0], pnc=a[1])

    def land(c, k):
        return T.R if (c % 8 not in GW and k % 2) else T.L

    def own_r(k):
        d = ob + SERVER.index(i)
        g.dma_start(T.R[:, :, 4 * i:4 * i + 4], T.x[k, :, 4 * d:4 * d + 8]).then_inc(sem.ownr, 16)

    nsig = 0
    nsent = 0
    g.dma_start(T.S[:], T.x[0]).then_inc(sem.ld, 16)
    if gw:
        own_r(0)
    kept = (3,) if gw else (2, 3)
    for k in kept:
        g.dma_start(land(core, k)[:, ch, 4 * i:4 * i + 4], T.x[k, :, own]).then_inc(sem.ownl, 16)
    for k in range(ROUNDS):
        g.wait_ge(sem.ld, 16 * (k + 1))
        if k:
            g.wait_ge(sem.rcred, ngw * k)
        tr = []
        for j in range(8):
            if SERVER[j] == i:
                continue
            d = ob + j
            tr.append(bass.RemoteDMATransfer(dst_ids=[dst(base + SERVER[j])], dma_engine_mask=3 << (2 * len(tr)),
                                             remote_sem=sem.rarr, src=T.S[:, 4 * d:4 * d + 4],
                                             dst=T.R[:, j % 2, 4 * i:4 * i + 4]))
        g.remote_dma_fused(tr, local_sem=sem.sent)
        nsent += 2 * len(tr)
        if k:
            g.wait_ge(sem.st, 16 * k)
            if gw:
                sg = [bass.RemoteDMATransfer(dst_ids=[dst(p)], dma_engine_mask=1 << (8 + n), remote_sem=sem.lcred)
                      for n, p in enumerate(peers)]
                sg.append(bass.RemoteDMATransfer(dst_ids=[dst(ob + SERVER[i])], dma_engine_mask=1, remote_sem=sem.xcred))
                if relay and k >= 2:
                    g.wait_ge(pst[k - 2], 2)
                    sg.append(bass.RemoteDMATransfer(dst_ids=[dst(ob + i)], dma_engine_mask=2, remote_sem=ycred[k - 2]))
                g.remote_dma_fused(sg, local_sem=sem.sig)
                nsig += len(sg)
            elif k <= 2:
                a = topo.addr(base + SERVER[i])
                g.remote_sem_update(pst[k - 1], sem.sig, a[1], a[0], 1)
                nsig += 1
            g.wait_ge(sem.lcred, ngw * k)
        tr = [bass.RemoteDMATransfer(dst_ids=[dst(p)], dma_engine_mask=3 << (2 + 2 * n), remote_sem=oarr[k % 2],
                                     src=T.S[:, 4 * p:4 * p + 4], dst=land(p, k)[:, ch, 4 * i:4 * i + 4])
              for n, p in enumerate(peers)]
        g.remote_dma_fused(tr, local_sem=sem.sent)
        nsent += 14
        if gw:
            g.wait_ge(sem.rarr, 28 * (k + 1))
            g.wait_ge(sem.ownr, 16 * (k + 1))
            if relay:
                if k >= 2:
                    g.wait_ge(ycred[k - 2], 1)
            elif k:
                g.wait_ge(sem.xcred, 2 * k)
            d = ob + SERVER.index(i)
            tr = [bass.RemoteDMATransfer(dst_ids=[dst(d + h)], dma_engine_mask=0xF << (4 * h), remote_sem=xarr[k % 2],
                                         src=T.R[:, h, :], dst=land(d + h, k)[:, ch, :]) for h in range(2)]
            g.remote_dma_fused(tr, local_sem=sem.x2l)
        if k == kept[0]:
            g.dma_start(T.y[0:k, :, own], T.x[0:k, :, own]).then_inc(sem.fix, 16)
        g.wait_ge(sem.sent, nsent)
        if k + 1 < ROUNDS:
            g.dma_start(T.S[:], T.x[k + 1]).then_inc(sem.ld, 16)
        if gw:
            g.wait_ge(sem.x2l, 8 * (k + 1))
            if k + 1 < ROUNDS:
                g.remote_dma_fused([bass.RemoteDMATransfer(dst_ids=[dst(p)], dma_engine_mask=1 << n, remote_sem=sem.rcred)
                                    for n, p in enumerate(peers)], local_sem=sem.sig)
                nsig += 7
        g.wait_ge(oarr[k % 2], 14 * (k // 2 + 1))
        g.wait_ge(xarr[k % 2], 4 * (k // 2 + 1))
        if k == 0:
            g.wait_ge(sem.ownl, 16 * len(kept))
        g.dma_start(T.y[k], land(core, k)[:]).then_inc(sem.st, 16)
        if gw and k + 1 < ROUNDS:
            own_r(k + 1)
    g.wait_ge(sem.st, 16 * ROUNDS)
    g.wait_ge(sem.fix, 16)
    g.wait_ge(sem.sig, nsig)
